import numpy as np
import ml_dtypes


def mxq(x, axis, fmt="e4m3"):
    dtype, down = {"e4m3": (ml_dtypes.float8_e4m3fn, 7), "e5m2": (ml_dtypes.float8_e5m2, 14)}[fmt]
    v = np.moveaxis(np.asarray(x, np.float32).astype(ml_dtypes.bfloat16).astype(np.float64), axis, -1)
    blocks = v.reshape(v.shape[:-1] + (-1, 32))
    amax = np.abs(blocks).max(-1, keepdims=True)
    byte = np.maximum(np.where(amax > 0, np.frexp(amax)[1] - 1 + 127, 0) - down, 1)
    scale = np.exp2(byte - 127.0)
    codes = (blocks / scale).astype(np.float32).astype(dtype).astype(np.float64)
    return np.moveaxis((codes * scale).reshape(v.shape), -1, axis)


WIDE = False


def mx_kscale(k):
    if not WIDE:
        return np.ones(k)
    levels = np.array([10, -10, 5, -5, 0])
    if k % 512:
        return np.exp2(np.random.permutation(np.resize(levels, k // 32))).repeat(32)
    a = np.empty((k // 512, 16))
    for p in range(k // 512):
        a[p, :8] = np.random.permutation(np.resize(levels, 8))
        for g in range(8):
            far = levels[np.abs(levels - a[p, g]) >= 10]
            a[p, g + 8] = far[np.random.randint(len(far))]
    return np.exp2(a.ravel()).repeat(32)


def f64(x):
    return np.asarray(x).astype(np.float64)


def striped8(idx):
    return np.asarray(idx).reshape(8, -1, 16).transpose(0, 2, 1).reshape(128, -1).astype(np.uint16)


def unstriped8(offs):
    return offs.reshape(8, 16, -1).transpose(0, 2, 1).reshape(8, -1).astype(np.int64)


def pick8(x, idx, run):
    r = np.arange(len(x))
    return x[r[:, None], idx[r % (8 * run) // run]]


E2M1 = np.array([0.0, 0.5, 1.0, 1.5, 2.0, 3.0, 4.0, 6.0, -0.0, -0.5, -1.0, -1.5, -2.0, -3.0, -4.0, -6.0])


def pack_weight(w, fmt):
    k, n = w.shape
    w = f64(np.asarray(w, np.float32).astype(ml_dtypes.bfloat16)).reshape(k // 32, 32, n)
    amax = np.abs(w).max(1)
    if fmt == "e4m3":
        byte = np.frexp(amax)[1] - 1 + 127 - 7
    else:
        mant, ex = np.frexp(amax / 6.0)
        byte = np.where(mant > 0.5, ex, ex - 1) + 127
    byte = np.clip(np.where(amax > 0, byte, 1), 1, 254)
    scaled = (w * np.exp2(127.0 - byte)[:, None, :]).reshape(k, n).astype(np.float32)
    by_word = np.ascontiguousarray(scaled.reshape(k // 512, 128, 4, n).transpose(0, 1, 3, 2))
    if fmt == "e4m3":
        words = by_word.astype(ml_dtypes.float8_e4m3fn).view(np.uint8)
    else:
        c = by_word.astype(ml_dtypes.float4_e2m1fn).view(np.uint8) & 0xF
        words = (c[..., 0::2] | (c[..., 1::2] << 4)).reshape(k // 512, 128, 2 * n)
    return np.ascontiguousarray(words), np.ascontiguousarray(byte.astype(np.uint8).reshape(k // 512, 16, n))


def unpack_weight(words, scales, fmt):
    g, _, n = scales.shape
    words = np.ascontiguousarray(words).reshape(g, 128, n, -1)
    if fmt == "e4m3":
        vals = words.view(ml_dtypes.float8_e4m3fn).astype(np.float64)
    else:
        nib = np.empty((g, 128, n, 4), np.uint8)
        nib[..., 0::2] = words & 0xF
        nib[..., 1::2] = words >> 4
        vals = E2M1[nib]
    vals = vals * np.repeat(np.exp2(scales.astype(np.float64) - 127.0), 8, axis=1)[..., None]
    return vals.transpose(0, 1, 3, 2).reshape(g * 512, n)


D, T, U, I, Q = 512, 1024, 1024, 512, 128


def setup_inputs():
    n = np.random.standard_normal
    idx = np.stack([np.random.permutation(T)[:I] for _ in range(8)])
    idx2 = np.stack([np.random.permutation(U)[:I] for _ in range(8)])
    idx3 = np.stack([np.random.permutation(T)[:I] for _ in range(8)])
    idx4 = np.stack([np.random.permutation(U)[:I] for _ in range(8)])
    idx5 = np.stack([np.random.permutation(U)[:I] for _ in range(8)])
    fd = mx_kscale(D)
    keysp = pack_weight(n((D, T)) / fd[:, None], "e4m3")
    notesp = pack_weight(n((D, U)) / fd[:, None], "e2m1")
    return {
        "query": (n((D, Q)) * 1.0 / np.sqrt(D) * fd[:, None]).astype(np.float32),
        "keys_words": keysp[0],
        "keys_scales": keysp[1],
        "notes_words": notesp[0],
        "notes_scales": notesp[1],
        "offs": striped8(idx),
        "offs2": striped8(idx2),
        "offs3": striped8(idx3),
        "offs4": striped8(idx4),
        "offs5": striped8(idx5),
    }


def reference(query, keys_words, keys_scales, notes_words, notes_scales, offs, offs2, offs3, offs4, offs5):
    idx = unstriped8(offs)
    idx2 = unstriped8(offs2)
    idx3 = unstriped8(offs3)
    idx4 = unstriped8(offs4)
    idx5 = unstriped8(offs5)
    keysu = unpack_weight(keys_words, keys_scales, "e4m3")
    notesu = unpack_weight(notes_words, notes_scales, "e2m1")
    queryq = mxq(f64(query), 0, "e4m3")
    a = queryq.T @ keysu
    b = queryq.T @ notesu
    f1 = np.zeros((Q, T))
    f1[np.arange(Q)[:, None], idx[np.arange(Q) % 128 // 16]] = pick8(b, idx2, 16)
    aa = np.maximum(a, f1)
    v = pick8(aa, idx3, 16) - pick8(b, idx4, 16)
    f2 = np.zeros((Q, U))
    f2[np.arange(Q)[:, None], idx2[np.arange(Q) % 128 // 16]] = v
    bb = b + f2
    y = pick8(bb, idx5, 16)
    return y

@@ -1,0 +1,128 @@
+from contextlib import ExitStack
+
+import concourse.mybir as mybir
+
+D, T, U, I, Q = 512, 1024, 1024, 512, 128
+FLOPS = 2 * D * Q * (T + U)
+
+F32 = mybir.dt.float32
+BF16 = mybir.dt.bfloat16
+I32 = mybir.dt.int32
+U32 = mybir.dt.uint32
+U16 = mybir.dt.uint16
+U8 = mybir.dt.uint8
+FP8X4 = mybir.dt.float8_e4m3fn_x4
+FP4X4 = mybir.dt.float4_e2m1fn_x4
+ALU = mybir.AluOpType
+COPY = mybir.ActivationFunctionType.Copy
+
+P = 128
+PACK = 4
+HALF = I // 2
+B_WIDTHS = (256, 256, 256, 128, 128)
+NA = 512
+
+
+def tile_attend_filledin_two_kernel(tc, query, keys_words, keys_scales, notes_words, notes_scales,
+                                     offs, offs2, offs3, offs4, offs5, out):
+    nc = tc.nc
+    with ExitStack() as ctx:
+        lists = ctx.enter_context(tc.tile_pool(name="lists", bufs=1))
+        keep = ctx.enter_context(tc.tile_pool(name="keep", bufs=1))
+        psum = ctx.enter_context(tc.psum_pool(name="psum", bufs=1))
+
+        def load_list(src, name):
+            t = lists.tile([P, I // 16], U16, name=name)
+            nc.sync.dma_start(t[:], src)
+            return t
+
+        def load_scales(src, name):
+            plane = keep.tile([P, src.shape[2]], U8, name=name, align_bytes=64)
+            nc.vector.memset(plane[:].bitcast(U32), 0)
+            for quad in range(4):
+                nc.sync.dma_start(plane[32 * quad : 32 * quad + 4, :].bitcast(I32),
+                                  src[0, 4 * quad : 4 * quad + 4, :].bitcast(I32))
+            return plane
+
+        def first(t):
+            return t[:, 0 : HALF // 16]
+
+        def second(t):
+            return t[:, HALF // 16 : I // 16]
+
+        q_raw = keep.tile([P, PACK, Q], F32, name="q_raw", tag="staged", align_bytes=64)
+        nc.sync.dma_start(q_raw[:], query.rearrange("(p j) q -> p j q", j=PACK))
+        n_words = keep.tile([P, 2 * U], U8, name="n_words", align_bytes=64)
+        nc.sync.dma_start(n_words[:].bitcast(I32), notes_words[0].bitcast(I32))
+        n_scales = load_scales(notes_scales, "n_scales")
+        o2 = load_list(offs2, "o2")
+        o1 = load_list(offs, "o1")
+
+        q_bf = keep.tile([P, Q, PACK], BF16, name="q_bf", tag="rounded", align_bytes=64)
+        nc.vector.tensor_copy(q_bf[:], q_raw[:].rearrange("p j q -> p q j"))
+        q_codes = keep.tile([P, Q], U32, name="q_codes", align_bytes=64)
+        q_scales = keep.tile([P, Q], U8, name="q_scales", align_bytes=64)
+        nc.vector.quantize_mx(out=q_codes[:].bitcast(FP8X4), scales=q_scales[:],
+                              in_=q_bf[:].rearrange("p q j -> p (q j)"))
+
+        o4 = load_list(offs4, "o4")
+        k_scales = load_scales(keys_scales, "k_scales")
+        k_words = keep.tile([P, T], U32, name="k_words", tag="staged", align_bytes=64)
+        nc.sync.dma_start(k_words[:].bitcast(I32), keys_words[0].rearrange("p t r -> p (t r)").bitcast(I32))
+        o3 = load_list(offs3, "o3")
+        o5 = load_list(offs5, "o5")
+
+        f1 = keep.tile([P, T], F32, name="f1")
+        nc.vector.memset(f1[:], 0.0)
+        f2 = keep.tile([P, U], F32, name="f2", tag="rounded", align_bytes=64)
+        nc.vector.memset(f2[:], 0.0)
+
+        b = keep.tile([P, U], F32, name="b")
+        for c, width in enumerate(B_WIDTHS):
+            n0 = sum(B_WIDTHS[:c])
+            cols = slice(n0, n0 + width)
+            bank = psum.tile([P, width], F32, name=f"b_bank{c}")
+            nc.tensor.matmul_mx(out=bank[:], lhsT=q_codes[:].bitcast(FP8X4), lhsT_scale=q_scales[:],
+                                rhs=n_words[:, 2 * n0 : 2 * (n0 + width)].bitcast(FP4X4),
+                                rhs_scale=n_scales[:, cols], start=True, stop=True)
+            if c % 2 == 0:
+                nc.scalar.activation(b[:, cols], bank[:], COPY)
+            else:
+                nc.vector.tensor_copy(b[:, cols], bank[:])
+
+        a_banks = []
+        for c in range(T // NA):
+            cols = slice(c * NA, (c + 1) * NA)
+            bank = psum.tile([P, NA], F32, name=f"a_bank{c}")
+            nc.tensor.matmul_mx(out=bank[:], lhsT=q_codes[:].bitcast(FP8X4), lhsT_scale=q_scales[:],
+                                rhs=k_words[:, cols].bitcast(FP8X4),
+                                rhs_scale=k_scales[:, cols], start=True, stop=True)
+            a_banks.append(bank)
+
+        g2 = keep.tile([P, I], F32, name="g2")
+        nc.vector.tensor_copy(g2[:, 0:HALF], b[:].indirect(first(o2)))
+        nc.scalar.activation(g2[:, HALF:I], b[:].indirect(second(o2)), COPY)
+        nc.vector.tensor_copy(f1[:].indirect(o1[:]), g2[:])
+
+        neg4 = keep.tile([P, I], F32, name="neg4")
+        nc.scalar.activation(neg4[:], b[:].indirect(o4[:]), COPY, scale=-1.0)
+
+        aa = keep.tile([P, T], F32, name="aa")
+        for c in range(T // NA):
+            cols = slice(c * NA, (c + 1) * NA)
+            nc.vector.tensor_tensor(aa[:, cols], a_banks[c][:], f1[:, cols], ALU.max)
+
+        g3 = keep.tile([P, I], F32, name="g3")
+        nc.vector.tensor_copy(g3[:, 0:HALF], aa[:].indirect(first(o3)))
+        nc.scalar.activation(g3[:, HALF:I], aa[:].indirect(second(o3)), COPY)
+        nc.vector.tensor_tensor(f2[:].indirect(o2[:]), g3[:], neg4[:], ALU.add)
+
+        bb = keep.tile([P, U], F32, name="bb")
+        nc.vector.tensor_tensor(bb[:], b[:], f2[:], ALU.add)
+
+        ya = keep.tile([P, HALF], F32, name="ya")
+        yb = keep.tile([P, HALF], F32, name="yb")
+        nc.vector.tensor_copy(ya[:], bb[:].indirect(first(o5)))
+        nc.scalar.activation(yb[:], bb[:].indirect(second(o5)), COPY)
+        nc.sync.dma_start(out[:, 0:HALF], ya[:])
+        nc.scalar.dma_start(out[:, HALF:I], yb[:])

@@ -78,6 +78,7 @@ def tile_attend_filledin_two_kernel(tc, query, keys_words, keys_scales, notes_wo
         nc.vector.memset(f2[:], 0.0)
 
         b = keep.tile([P, U], F32, name="b")
+        b_banks = []
         for c, width in enumerate(B_WIDTHS):
             n0 = sum(B_WIDTHS[:c])
             cols = slice(n0, n0 + width)
@@ -85,6 +86,7 @@ def tile_attend_filledin_two_kernel(tc, query, keys_words, keys_scales, notes_wo
             nc.tensor.matmul_mx(out=bank[:], lhsT=q_codes[:].bitcast(FP8X4), lhsT_scale=q_scales[:],
                                 rhs=n_words[:, 2 * n0 : 2 * (n0 + width)].bitcast(FP4X4),
                                 rhs_scale=n_scales[:, cols], start=True, stop=True)
+            b_banks.append((cols, bank))
             if c % 2 == 0:
                 nc.scalar.activation(b[:, cols], bank[:], COPY)
             else:
@@ -118,7 +120,10 @@ def tile_attend_filledin_two_kernel(tc, query, keys_words, keys_scales, notes_wo
         nc.vector.tensor_tensor(f2[:].indirect(o2[:]), g3[:], neg4[:], ALU.add)
 
         bb = keep.tile([P, U], F32, name="bb")
-        nc.vector.tensor_tensor(bb[:], b[:], f2[:], ALU.add)
+        for cols, bank in b_banks[:3]:
+            nc.vector.tensor_tensor(bb[:, cols], bank[:], f2[:, cols], ALU.add)
+        rest = slice(sum(B_WIDTHS[:3]), U)
+        nc.gpsimd.tensor_tensor(bb[:, rest], b[:, rest], f2[:, rest], ALU.add)
 
         ya = keep.tile([P, HALF], F32, name="ya")
         yb = keep.tile([P, HALF], F32, name="yb")

@@ -38,7 +38,6 @@ def tile_attend_filledin_two_kernel(tc, query, keys_words, keys_scales, notes_wo
 
         def load_scales(src, name):
             plane = keep.tile([P, src.shape[2]], U8, name=name, align_bytes=64)
-            nc.vector.memset(plane[:].bitcast(U32), 0)
             for quad in range(4):
                 nc.sync.dma_start(plane[32 * quad : 32 * quad + 4, :].bitcast(I32),
                                   src[0, 4 * quad : 4 * quad + 4, :].bitcast(I32))
@@ -50,25 +49,35 @@ def tile_attend_filledin_two_kernel(tc, query, keys_words, keys_scales, notes_wo
         def second(t):
             return t[:, HALF // 16 : I // 16]
 
-        q_raw = keep.tile([P, PACK, Q], F32, name="q_raw", tag="staged", align_bytes=64)
+        q_raw = keep.tile([P, PACK, Q], F32, name="q_raw", align_bytes=64)
         nc.sync.dma_start(q_raw[:], query.rearrange("(p j) q -> p j q", j=PACK))
-        n_words = keep.tile([P, 2 * U], U8, name="n_words", align_bytes=64)
-        nc.sync.dma_start(n_words[:].bitcast(I32), notes_words[0].bitcast(I32))
         n_scales = load_scales(notes_scales, "n_scales")
+        n_words = keep.tile([P, 2 * U], U8, name="n_words", align_bytes=64)
+        for half in (slice(0, U), slice(U, 2 * U)):
+            nc.sync.dma_start(n_words[:, half].bitcast(I32), notes_words[0, :, half].bitcast(I32))
         o2 = load_list(offs2, "o2")
         o1 = load_list(offs, "o1")
 
         q_bf = keep.tile([P, Q, PACK], BF16, name="q_bf", tag="rounded", align_bytes=64)
-        nc.vector.tensor_copy(q_bf[:], q_raw[:].rearrange("p j q -> p q j"))
+        def runs_out(cols):
+            return q_bf[:, cols, :].rearrange("p (c i) j -> p c j i", i=4)
+
+        def runs_in(cols):
+            return q_raw[:, :, cols].rearrange("p j (c i) -> p c j i", i=4)
+
+        for cols in (slice(0, 64), slice(64, 96)):
+            nc.vector.tensor_copy(runs_out(cols), runs_in(cols))
+        nc.scalar.activation(runs_out(slice(96, Q)), runs_in(slice(96, Q)), COPY)
         q_codes = keep.tile([P, Q], U32, name="q_codes", align_bytes=64)
         q_scales = keep.tile([P, Q], U8, name="q_scales", align_bytes=64)
-        nc.vector.quantize_mx(out=q_codes[:].bitcast(FP8X4), scales=q_scales[:],
-                              in_=q_bf[:].rearrange("p q j -> p (q j)"))
+        for cols in (slice(0, 64), slice(64, Q)):
+            nc.vector.quantize_mx(out=q_codes[:, cols].bitcast(FP8X4), scales=q_scales[:, cols],
+                                  in_=q_bf[:, cols, :].rearrange("p q j -> p (q j)"))
 
+        k_words = keep.tile([P, T], U32, name="k_words", align_bytes=64)
+        nc.sync.dma_start(k_words[:].bitcast(I32), keys_words[0].rearrange("p t r -> p (t r)").bitcast(I32))
         o4 = load_list(offs4, "o4")
         k_scales = load_scales(keys_scales, "k_scales")
-        k_words = keep.tile([P, T], U32, name="k_words", tag="staged", align_bytes=64)
-        nc.sync.dma_start(k_words[:].bitcast(I32), keys_words[0].rearrange("p t r -> p (t r)").bitcast(I32))
         o3 = load_list(offs3, "o3")
         o5 = load_list(offs5, "o5")
 

@@ -38,9 +38,8 @@ def tile_attend_filledin_two_kernel(tc, query, keys_words, keys_scales, notes_wo
 
         def load_scales(src, name):
             plane = keep.tile([P, src.shape[2]], U8, name=name, align_bytes=64)
-            for quad in range(4):
-                nc.sync.dma_start(plane[32 * quad : 32 * quad + 4, :].bitcast(I32),
-                                  src[0, 4 * quad : 4 * quad + 4, :].bitcast(I32))
+            for r in range(4):
+                nc.sync.dma_start(plane[r:P:32, :].bitcast(I32), src[0, r:16:4, :].bitcast(I32))
             return plane
 
         def first(t):
@@ -58,7 +57,7 @@ def tile_attend_filledin_two_kernel(tc, query, keys_words, keys_scales, notes_wo
         o2 = load_list(offs2, "o2")
         o1 = load_list(offs, "o1")
 
-        q_bf = keep.tile([P, Q, PACK], BF16, name="q_bf", tag="rounded", align_bytes=64)
+        q_bf = keep.tile([P, Q, PACK], BF16, name="q_bf", align_bytes=64)
         def runs_out(cols):
             return q_bf[:, cols, :].rearrange("p (c i) j -> p c j i", i=4)
 
@@ -83,7 +82,7 @@ def tile_attend_filledin_two_kernel(tc, query, keys_words, keys_scales, notes_wo
 
         f1 = keep.tile([P, T], F32, name="f1")
         nc.vector.memset(f1[:], 0.0)
-        f2 = keep.tile([P, U], F32, name="f2", tag="rounded", align_bytes=64)
+        f2 = keep.tile([P, U], F32, name="f2")
         nc.vector.memset(f2[:], 0.0)
 
         b = keep.tile([P, U], F32, name="b")

@@ -36,11 +36,9 @@ def tile_attend_filledin_two_kernel(tc, query, keys_words, keys_scales, notes_wo
             nc.sync.dma_start(t[:], src)
             return t
 
-        def load_scales(src, name):
-            plane = keep.tile([P, src.shape[2]], U8, name=name, align_bytes=64)
-            for r in range(4):
-                nc.sync.dma_start(plane[r:P:32, :].bitcast(I32), src[0, r:16:4, :].bitcast(I32))
-            return plane
+        def load_scale_rows(queue, plane, src, rows):
+            for r in rows:
+                queue.dma_start(plane[r:P:32, :].bitcast(I32), src[0, r:16:4, :].bitcast(I32))
 
         def first(t):
             return t[:, 0 : HALF // 16]
@@ -50,10 +48,12 @@ def tile_attend_filledin_two_kernel(tc, query, keys_words, keys_scales, notes_wo
 
         q_raw = keep.tile([P, PACK, Q], F32, name="q_raw", align_bytes=64)
         nc.sync.dma_start(q_raw[:], query.rearrange("(p j) q -> p j q", j=PACK))
-        n_scales = load_scales(notes_scales, "n_scales")
+        n_scales = keep.tile([P, U], U8, name="n_scales", align_bytes=64)
         n_words = keep.tile([P, 2 * U], U8, name="n_words", align_bytes=64)
-        for half in (slice(0, U), slice(U, 2 * U)):
-            nc.sync.dma_start(n_words[:, half].bitcast(I32), notes_words[0, :, half].bitcast(I32))
+        load_scale_rows(nc.scalar, n_scales, notes_scales, (0, 1))
+        nc.sync.dma_start(n_words[:, 0:U].bitcast(I32), notes_words[0, :, 0:U].bitcast(I32))
+        load_scale_rows(nc.sync, n_scales, notes_scales, (2, 3))
+        nc.sync.dma_start(n_words[:, U : 2 * U].bitcast(I32), notes_words[0, :, U : 2 * U].bitcast(I32))
         o2 = load_list(offs2, "o2")
         o1 = load_list(offs, "o1")
 
@@ -76,7 +76,8 @@ def tile_attend_filledin_two_kernel(tc, query, keys_words, keys_scales, notes_wo
         k_words = keep.tile([P, T], U32, name="k_words", align_bytes=64)
         nc.sync.dma_start(k_words[:].bitcast(I32), keys_words[0].rearrange("p t r -> p (t r)").bitcast(I32))
         o4 = load_list(offs4, "o4")
-        k_scales = load_scales(keys_scales, "k_scales")
+        k_scales = keep.tile([P, T], U8, name="k_scales", align_bytes=64)
+        load_scale_rows(nc.sync, k_scales, keys_scales, range(4))
         o3 = load_list(offs3, "o3")
         o5 = load_list(offs5, "o5")
 

from contextlib import ExitStack

import concourse.mybir as mybir

D, T, U, I, Q = 512, 1024, 1024, 512, 128
FLOPS = 2 * D * Q * (T + U)

F32 = mybir.dt.float32
BF16 = mybir.dt.bfloat16
I32 = mybir.dt.int32
U32 = mybir.dt.uint32
U16 = mybir.dt.uint16
U8 = mybir.dt.uint8
FP8X4 = mybir.dt.float8_e4m3fn_x4
FP4X4 = mybir.dt.float4_e2m1fn_x4
ALU = mybir.AluOpType
COPY = mybir.ActivationFunctionType.Copy

P = 128
PACK = 4
HALF = I // 2
B_WIDTHS = (256, 256, 256, 128, 128)
NA = 512


def tile_attend_filledin_two_kernel(tc, query, keys_words, keys_scales, notes_words, notes_scales,
                                     offs, offs2, offs3, offs4, offs5, out):
    nc = tc.nc
    with ExitStack() as ctx:
        lists = ctx.enter_context(tc.tile_pool(name="lists", bufs=1))
        keep = ctx.enter_context(tc.tile_pool(name="keep", bufs=1))
        psum = ctx.enter_context(tc.psum_pool(name="psum", bufs=1))

        def load_list(src, name):
            t = lists.tile([P, I // 16], U16, name=name)
            nc.sync.dma_start(t[:], src)
            return t

        def load_scale_rows(queue, plane, src, rows):
            for r in rows:
                queue.dma_start(plane[r:P:32, :].bitcast(I32), src[0, r:16:4, :].bitcast(I32))

        def first(t):
            return t[:, 0 : HALF // 16]

        def second(t):
            return t[:, HALF // 16 : I // 16]

        q_raw = keep.tile([P, PACK, Q], F32, name="q_raw", align_bytes=64)
        nc.sync.dma_start(q_raw[:], query.rearrange("(p j) q -> p j q", j=PACK))
        n_scales = keep.tile([P, U], U8, name="n_scales", align_bytes=64)
        n_words = keep.tile([P, 2 * U], U8, name="n_words", align_bytes=64)
        load_scale_rows(nc.scalar, n_scales, notes_scales, (0, 1))
        nc.sync.dma_start(n_words[:, 0:U].bitcast(I32), notes_words[0, :, 0:U].bitcast(I32))
        load_scale_rows(nc.sync, n_scales, notes_scales, (2, 3))
        nc.sync.dma_start(n_words[:, U : 2 * U].bitcast(I32), notes_words[0, :, U : 2 * U].bitcast(I32))
        o2 = load_list(offs2, "o2")
        o1 = load_list(offs, "o1")

        q_bf = keep.tile([P, Q, PACK], BF16, name="q_bf", align_bytes=64)
        def runs_out(cols):
            return q_bf[:, cols, :].rearrange("p (c i) j -> p c j i", i=4)

        def runs_in(cols):
            return q_raw[:, :, cols].rearrange("p j (c i) -> p c j i", i=4)

        for cols in (slice(0, 64), slice(64, 96)):
            nc.vector.tensor_copy(runs_out(cols), runs_in(cols))
        nc.scalar.activation(runs_out(slice(96, Q)), runs_in(slice(96, Q)), COPY)
        q_codes = keep.tile([P, Q], U32, name="q_codes", align_bytes=64)
        q_scales = keep.tile([P, Q], U8, name="q_scales", align_bytes=64)
        for cols in (slice(0, 64), slice(64, Q)):
            nc.vector.quantize_mx(out=q_codes[:, cols].bitcast(FP8X4), scales=q_scales[:, cols],
                                  in_=q_bf[:, cols, :].rearrange("p q j -> p (q j)"))

        k_words = keep.tile([P, T], U32, name="k_words", align_bytes=64)
        nc.sync.dma_start(k_words[:].bitcast(I32), keys_words[0].rearrange("p t r -> p (t r)").bitcast(I32))
        o4 = load_list(offs4, "o4")
        k_scales = keep.tile([P, T], U8, name="k_scales", align_bytes=64)
        load_scale_rows(nc.sync, k_scales, keys_scales, range(4))
        o3 = load_list(offs3, "o3")
        o5 = load_list(offs5, "o5")

        f1 = keep.tile([P, T], F32, name="f1")
        nc.vector.memset(f1[:], 0.0)
        f2 = keep.tile([P, U], F32, name="f2")
        nc.vector.memset(f2[:], 0.0)

        b = keep.tile([P, U], F32, name="b")
        b_banks = []
        for c, width in enumerate(B_WIDTHS):
            n0 = sum(B_WIDTHS[:c])
            cols = slice(n0, n0 + width)
            bank = psum.tile([P, width], F32, name=f"b_bank{c}")
            nc.tensor.matmul_mx(out=bank[:], lhsT=q_codes[:].bitcast(FP8X4), lhsT_scale=q_scales[:],
                                rhs=n_words[:, 2 * n0 : 2 * (n0 + width)].bitcast(FP4X4),
                                rhs_scale=n_scales[:, cols], start=True, stop=True)
            b_banks.append((cols, bank))
            if c % 2 == 0:
                nc.scalar.activation(b[:, cols], bank[:], COPY)
            else:
                nc.vector.tensor_copy(b[:, cols], bank[:])

        a_banks = []
        for c in range(T // NA):
            cols = slice(c * NA, (c + 1) * NA)
            bank = psum.tile([P, NA], F32, name=f"a_bank{c}")
            nc.tensor.matmul_mx(out=bank[:], lhsT=q_codes[:].bitcast(FP8X4), lhsT_scale=q_scales[:],
                                rhs=k_words[:, cols].bitcast(FP8X4),
                                rhs_scale=k_scales[:, cols], start=True, stop=True)
            a_banks.append(bank)

        g2 = keep.tile([P, I], F32, name="g2")
        nc.vector.tensor_copy(g2[:, 0:HALF], b[:].indirect(first(o2)))
        nc.scalar.activation(g2[:, HALF:I], b[:].indirect(second(o2)), COPY)
        nc.vector.tensor_copy(f1[:].indirect(o1[:]), g2[:])

        neg4 = keep.tile([P, I], F32, name="neg4")
        nc.scalar.activation(neg4[:], b[:].indirect(o4[:]), COPY, scale=-1.0)

        aa = keep.tile([P, T], F32, name="aa")
        for c in range(T // NA):
            cols = slice(c * NA, (c + 1) * NA)
            nc.vector.tensor_tensor(aa[:, cols], a_banks[c][:], f1[:, cols], ALU.max)

        g3 = keep.tile([P, I], F32, name="g3")
        nc.vector.tensor_copy(g3[:, 0:HALF], aa[:].indirect(first(o3)))
        nc.scalar.activation(g3[:, HALF:I], aa[:].indirect(second(o3)), COPY)
        nc.vector.tensor_tensor(f2[:].indirect(o2[:]), g3[:], neg4[:], ALU.add)

        bb = keep.tile([P, U], F32, name="bb")
        for cols, bank in b_banks[:3]:
            nc.vector.tensor_tensor(bb[:, cols], bank[:], f2[:, cols], ALU.add)
        rest = slice(sum(B_WIDTHS[:3]), U)
        nc.gpsimd.tensor_tensor(bb[:, rest], b[:, rest], f2[:, rest], ALU.add)

        ya = keep.tile([P, HALF], F32, name="ya")
        yb = keep.tile([P, HALF], F32, name="yb")
        nc.vector.tensor_copy(ya[:], bb[:].indirect(first(o5)))
        nc.scalar.activation(yb[:], bb[:].indirect(second(o5)), COPY)
        nc.sync.dma_start(out[:, 0:HALF], ya[:])
        nc.scalar.dma_start(out[:, HALF:I], yb[:])
